import numpy as np
import ml_dtypes

BF16 = ml_dtypes.bfloat16


def bf(x):
    return np.asarray(x, np.float32).astype(BF16)


def f32(x):
    return np.asarray(x, np.float32)


def f64(x):
    return np.asarray(x).astype(np.float64)


def striped(idx):
    return np.tile(idx.reshape(-1, 16).T, (8, 1))


S, K, M, N, D, V = 1024, 128, 256, 1536, 16, 96


def setup_inputs():
    return {"table": bf(np.random.standard_normal((K, S))), "w": bf(np.random.standard_normal((K, M)) / np.sqrt(K)), "b": f32(0.5 * np.random.standard_normal((M, 1))), "offs": striped(np.random.permutation(np.tile(np.arange(S), 2))[:N])}


def reference(table, w, b, offs):
    idx = offs[:16].T.reshape(-1)
    x = f64(table)[:, idx]
    y = f64(w).T @ x
    z = np.maximum(y + f64(b), 0.0)
    return z.reshape(M, V, D).max(axis=2)

@@ -1,0 +1,58 @@
+import concourse.mybir as mybir
+
+BF16, F32, U16 = mybir.dt.bfloat16, mybir.dt.float32, mybir.dt.uint16
+ADD, MAX = mybir.AluOpType.add, mybir.AluOpType.max
+
+P = 128
+S = 1024
+M = 256
+N = 1536
+GROUP = 16
+PIECE = 512
+PER_COLUMN = 16
+
+M_BLOCKS = M // P
+PIECES = N // PIECE
+PIECE_COLUMNS = PIECE // PER_COLUMN
+PIECE_NODES = PIECE // GROUP
+NODES = N // GROUP
+
+FLOPS = 2 * P * M * N
+
+
+def tile_gather_matmul_kernel(tc, table, w, b, offs, out):
+    nc = tc.nc
+    with (
+        tc.tile_pool(name="held", bufs=1) as held,
+        tc.psum_pool(name="banks", bufs=M_BLOCKS * PIECES) as banks,
+    ):
+        offsets = held.tile([P, N // PER_COLUMN], U16, name="offsets")
+        nc.sync.dma_start(offsets[:], offs)
+        nodes = held.tile([P, S], BF16, name="nodes")
+        nc.scalar.dma_start(nodes[:], table)
+        weights = held.tile([P, M], BF16, name="weights")
+        nc.sync.dma_start(weights[:], w)
+        bias = held.tile([P, M_BLOCKS], F32, name="bias")
+        with nc.allow_non_contiguous_dma(reason="256 single floats, one to a partition and block"):
+            nc.scalar.dma_start(bias[:], b.rearrange("(a p) o -> p (a o)", p=P))
+
+        for a in range(M_BLOCKS):
+            largest = held.tile([P, NODES], F32, name=f"largest{a}")
+            for q in range(PIECES):
+                product = banks.tile([P, PIECE], F32, name="product")
+                nc.tensor.matmul(
+                    product[:],
+                    weights[:, a * P : (a + 1) * P],
+                    nodes[:].indirect(offsets[:, q * PIECE_COLUMNS : (q + 1) * PIECE_COLUMNS]),
+                    start=True,
+                    stop=True,
+                )
+                nc.vector.tensor_reduce(
+                    largest[:, q * PIECE_NODES : (q + 1) * PIECE_NODES],
+                    product[:].rearrange("p (v t) -> p v t", t=GROUP),
+                    axis=mybir.AxisListType.X,
+                    op=MAX,
+                )
+            pooled = held.tile([P, NODES], F32, name=f"pooled{a}")
+            nc.vector.tensor_scalar(pooled[:], largest[:], bias[:, a : a + 1], 0.0, op0=ADD, op1=MAX)
+            nc.sync.dma_start(out[a * P : (a + 1) * P, :], pooled[:])

@@ -8,7 +8,8 @@ S = 1024
 M = 256
 N = 1536
 GROUP = 16
-PIECE = 512
+PIECE = 256
+PSUM_BANKS = 8
 PER_COLUMN = 16
 
 M_BLOCKS = M // P
@@ -24,7 +25,7 @@ def tile_gather_matmul_kernel(tc, table, w, b, offs, out):
     nc = tc.nc
     with (
         tc.tile_pool(name="held", bufs=1) as held,
-        tc.psum_pool(name="banks", bufs=M_BLOCKS * PIECES) as banks,
+        tc.psum_pool(name="banks", bufs=PSUM_BANKS) as banks,
     ):
         offsets = held.tile([P, N // PER_COLUMN], U16, name="offsets")
         nc.sync.dma_start(offsets[:], offs)

@@ -27,15 +27,15 @@ def tile_gather_matmul_kernel(tc, table, w, b, offs, out):
         tc.tile_pool(name="held", bufs=1) as held,
         tc.psum_pool(name="banks", bufs=PSUM_BANKS) as banks,
     ):
+        nodes = held.tile([P, S], BF16, name="nodes")
+        nc.sync.dma_start(nodes[:], table)
         offsets = held.tile([P, N // PER_COLUMN], U16, name="offsets")
         nc.sync.dma_start(offsets[:], offs)
-        nodes = held.tile([P, S], BF16, name="nodes")
-        nc.scalar.dma_start(nodes[:], table)
         weights = held.tile([P, M], BF16, name="weights")
         nc.sync.dma_start(weights[:], w)
         bias = held.tile([P, M_BLOCKS], F32, name="bias")
         with nc.allow_non_contiguous_dma(reason="256 single floats, one to a partition and block"):
-            nc.scalar.dma_start(bias[:], b.rearrange("(a p) o -> p (a o)", p=P))
+            nc.sync.dma_start(bias[:], b.rearrange("(a p) o -> p (a o)", p=P))
 
         for a in range(M_BLOCKS):
             largest = held.tile([P, NODES], F32, name=f"largest{a}")

@@ -32,10 +32,10 @@ def tile_gather_matmul_kernel(tc, table, w, b, offs, out):
         offsets = held.tile([P, N // PER_COLUMN], U16, name="offsets")
         nc.sync.dma_start(offsets[:], offs)
         weights = held.tile([P, M], BF16, name="weights")
-        nc.sync.dma_start(weights[:], w)
+        nc.scalar.dma_start(weights[:], w)
         bias = held.tile([P, M_BLOCKS], F32, name="bias")
         with nc.allow_non_contiguous_dma(reason="256 single floats, one to a partition and block"):
-            nc.sync.dma_start(bias[:], b.rearrange("(a p) o -> p (a o)", p=P))
+            nc.scalar.dma_start(bias[:], b.rearrange("(a p) o -> p (a o)", p=P))
 
         for a in range(M_BLOCKS):
             largest = held.tile([P, NODES], F32, name=f"largest{a}")

@@ -2,6 +2,7 @@ import concourse.mybir as mybir
 
 BF16, F32, U16 = mybir.dt.bfloat16, mybir.dt.float32, mybir.dt.uint16
 ADD, MAX = mybir.AluOpType.add, mybir.AluOpType.max
+RELU = mybir.ActivationFunctionType.Relu
 
 P = 128
 S = 1024
@@ -37,6 +38,11 @@ def tile_gather_matmul_kernel(tc, table, w, b, offs, out):
         with nc.allow_non_contiguous_dma(reason="256 single floats, one to a partition and block"):
             nc.scalar.dma_start(bias[:], b.rearrange("(a p) o -> p (a o)", p=P))
 
+        zeros = held.tile([P, 1], F32, name="zeros")
+        nc.vector.memset(zeros[:], 0.0)
+        warmed = held.tile([P, 1], F32, name="warmed")
+        nc.scalar.activation(warmed[:], zeros[:], RELU)
+
         for a in range(M_BLOCKS):
             largest = held.tile([P, NODES], F32, name=f"largest{a}")
             for q in range(PIECES):
@@ -55,5 +61,8 @@ def tile_gather_matmul_kernel(tc, table, w, b, offs, out):
                     op=MAX,
                 )
             pooled = held.tile([P, NODES], F32, name=f"pooled{a}")
-            nc.vector.tensor_scalar(pooled[:], largest[:], bias[:, a : a + 1], 0.0, op0=ADD, op1=MAX)
+            if a < M_BLOCKS - 1:
+                nc.scalar.activation(pooled[:], largest[:], RELU, bias=bias[:, a : a + 1])
+            else:
+                nc.vector.tensor_scalar(pooled[:], largest[:], bias[:, a : a + 1], 0.0, op0=ADD, op1=MAX)
             nc.sync.dma_start(out[a * P : (a + 1) * P, :], pooled[:])

@@ -17,7 +17,7 @@ M_BLOCKS = M // P
 PIECES = N // PIECE
 PIECE_COLUMNS = PIECE // PER_COLUMN
 PIECE_NODES = PIECE // GROUP
-NODES = N // GROUP
+LAST_PIECES = 2
 
 FLOPS = 2 * P * M * N
 
@@ -43,9 +43,14 @@ def tile_gather_matmul_kernel(tc, table, w, b, offs, out):
         warmed = held.tile([P, 1], F32, name="warmed")
         nc.scalar.activation(warmed[:], zeros[:], RELU)
 
-        for a in range(M_BLOCKS):
-            largest = held.tile([P, NODES], F32, name=f"largest{a}")
-            for q in range(PIECES):
+        parts = [(a, 0, PIECES) for a in range(M_BLOCKS - 1)]
+        parts.append((M_BLOCKS - 1, 0, PIECES - LAST_PIECES))
+        parts.append((M_BLOCKS - 1, PIECES - LAST_PIECES, LAST_PIECES))
+        for number, (a, first_piece, pieces) in enumerate(parts):
+            part_nodes = pieces * PIECE_NODES
+            largest = held.tile([P, part_nodes], F32, name=f"largest{number}")
+            for i in range(pieces):
+                q = first_piece + i
                 product = banks.tile([P, PIECE], F32, name="product")
                 nc.tensor.matmul(
                     product[:],
@@ -55,14 +60,15 @@ def tile_gather_matmul_kernel(tc, table, w, b, offs, out):
                     stop=True,
                 )
                 nc.vector.tensor_reduce(
-                    largest[:, q * PIECE_NODES : (q + 1) * PIECE_NODES],
+                    largest[:, i * PIECE_NODES : (i + 1) * PIECE_NODES],
                     product[:].rearrange("p (v t) -> p v t", t=GROUP),
                     axis=mybir.AxisListType.X,
                     op=MAX,
                 )
-            pooled = held.tile([P, NODES], F32, name=f"pooled{a}")
-            if a < M_BLOCKS - 1:
+            pooled = held.tile([P, part_nodes], F32, name=f"pooled{number}")
+            if number < len(parts) - 1:
                 nc.scalar.activation(pooled[:], largest[:], RELU, bias=bias[:, a : a + 1])
             else:
                 nc.vector.tensor_scalar(pooled[:], largest[:], bias[:, a : a + 1], 0.0, op0=ADD, op1=MAX)
-            nc.sync.dma_start(out[a * P : (a + 1) * P, :], pooled[:])
+            first_node = first_piece * PIECE_NODES
+            nc.sync.dma_start(out[a * P : (a + 1) * P, first_node : first_node + part_nodes], pooled[:])

@@ -17,7 +17,7 @@ M_BLOCKS = M // P
 PIECES = N // PIECE
 PIECE_COLUMNS = PIECE // PER_COLUMN
 PIECE_NODES = PIECE // GROUP
-LAST_PIECES = 2
+PART_PIECES = (4, 2)
 
 FLOPS = 2 * P * M * N
 
@@ -43,9 +43,12 @@ def tile_gather_matmul_kernel(tc, table, w, b, offs, out):
         warmed = held.tile([P, 1], F32, name="warmed")
         nc.scalar.activation(warmed[:], zeros[:], RELU)
 
-        parts = [(a, 0, PIECES) for a in range(M_BLOCKS - 1)]
-        parts.append((M_BLOCKS - 1, 0, PIECES - LAST_PIECES))
-        parts.append((M_BLOCKS - 1, PIECES - LAST_PIECES, LAST_PIECES))
+        parts = []
+        for a in range(M_BLOCKS):
+            first_piece = 0
+            for pieces in PART_PIECES:
+                parts.append((a, first_piece, pieces))
+                first_piece += pieces
         for number, (a, first_piece, pieces) in enumerate(parts):
             part_nodes = pieces * PIECE_NODES
             largest = held.tile([P, part_nodes], F32, name=f"largest{number}")

import concourse.mybir as mybir

BF16, F32, U16 = mybir.dt.bfloat16, mybir.dt.float32, mybir.dt.uint16
ADD, MAX = mybir.AluOpType.add, mybir.AluOpType.max
RELU = mybir.ActivationFunctionType.Relu

P = 128
S = 1024
M = 256
N = 1536
GROUP = 16
PIECE = 256
PSUM_BANKS = 8
PER_COLUMN = 16

M_BLOCKS = M // P
PIECES = N // PIECE
PIECE_COLUMNS = PIECE // PER_COLUMN
PIECE_NODES = PIECE // GROUP
PART_PIECES = (4, 2)

FLOPS = 2 * P * M * N


def tile_gather_matmul_kernel(tc, table, w, b, offs, out):
    nc = tc.nc
    with (
        tc.tile_pool(name="held", bufs=1) as held,
        tc.psum_pool(name="banks", bufs=PSUM_BANKS) as banks,
    ):
        nodes = held.tile([P, S], BF16, name="nodes")
        nc.sync.dma_start(nodes[:], table)
        offsets = held.tile([P, N // PER_COLUMN], U16, name="offsets")
        nc.sync.dma_start(offsets[:], offs)
        weights = held.tile([P, M], BF16, name="weights")
        nc.scalar.dma_start(weights[:], w)
        bias = held.tile([P, M_BLOCKS], F32, name="bias")
        with nc.allow_non_contiguous_dma(reason="256 single floats, one to a partition and block"):
            nc.scalar.dma_start(bias[:], b.rearrange("(a p) o -> p (a o)", p=P))

        zeros = held.tile([P, 1], F32, name="zeros")
        nc.vector.memset(zeros[:], 0.0)
        warmed = held.tile([P, 1], F32, name="warmed")
        nc.scalar.activation(warmed[:], zeros[:], RELU)

        parts = []
        for a in range(M_BLOCKS):
            first_piece = 0
            for pieces in PART_PIECES:
                parts.append((a, first_piece, pieces))
                first_piece += pieces
        for number, (a, first_piece, pieces) in enumerate(parts):
            part_nodes = pieces * PIECE_NODES
            largest = held.tile([P, part_nodes], F32, name=f"largest{number}")
            for i in range(pieces):
                q = first_piece + i
                product = banks.tile([P, PIECE], F32, name="product")
                nc.tensor.matmul(
                    product[:],
                    weights[:, a * P : (a + 1) * P],
                    nodes[:].indirect(offsets[:, q * PIECE_COLUMNS : (q + 1) * PIECE_COLUMNS]),
                    start=True,
                    stop=True,
                )
                nc.vector.tensor_reduce(
                    largest[:, i * PIECE_NODES : (i + 1) * PIECE_NODES],
                    product[:].rearrange("p (v t) -> p v t", t=GROUP),
                    axis=mybir.AxisListType.X,
                    op=MAX,
                )
            pooled = held.tile([P, part_nodes], F32, name=f"pooled{number}")
            if number < len(parts) - 1:
                nc.scalar.activation(pooled[:], largest[:], RELU, bias=bias[:, a : a + 1])
            else:
                nc.vector.tensor_scalar(pooled[:], largest[:], bias[:, a : a + 1], 0.0, op0=ADD, op1=MAX)
            first_node = first_piece * PIECE_NODES
            nc.sync.dma_start(out[a * P : (a + 1) * P, first_node : first_node + part_nodes], pooled[:])
